import numpy as np
import ml_dtypes


def mxq(x, axis, fmt="e4m3"):
    dtype, down = {"e4m3": (ml_dtypes.float8_e4m3fn, 7), "e5m2": (ml_dtypes.float8_e5m2, 14)}[fmt]
    v = np.moveaxis(np.asarray(x, np.float32).astype(ml_dtypes.bfloat16).astype(np.float64), axis, -1)
    blocks = v.reshape(v.shape[:-1] + (-1, 32))
    amax = np.abs(blocks).max(-1, keepdims=True)
    byte = np.maximum(np.where(amax > 0, np.frexp(amax)[1] - 1 + 127, 0) - down, 1)
    scale = np.exp2(byte - 127.0)
    codes = (blocks / scale).astype(np.float32).astype(dtype).astype(np.float64)
    return np.moveaxis((codes * scale).reshape(v.shape), -1, axis)


WIDE = False


def mx_kscale(k):
    if not WIDE:
        return np.ones(k)
    levels = np.array([10, -10, 5, -5, 0])
    if k % 512:
        return np.exp2(np.random.permutation(np.resize(levels, k // 32))).repeat(32)
    a = np.empty((k // 512, 16))
    for p in range(k // 512):
        a[p, :8] = np.random.permutation(np.resize(levels, 8))
        for g in range(8):
            far = levels[np.abs(levels - a[p, g]) >= 10]
            a[p, g + 8] = far[np.random.randint(len(far))]
    return np.exp2(a.ravel()).repeat(32)


def f64(x):
    return np.asarray(x).astype(np.float64)


def striped(idx):
    return np.tile(idx.reshape(-1, 16).T, (8, 1)).astype(np.uint16)


def unstriped(offs):
    return offs[:16].T.reshape(-1).astype(np.int64)


def pack_weight(w):
    k, n = w.shape
    w = f64(np.asarray(w, np.float32).astype(ml_dtypes.bfloat16)).reshape(k // 32, 32, n)
    amax = np.abs(w).max(1)
    byte = np.clip(np.where(amax > 0, np.frexp(amax)[1] - 1 + 127 - 7, 1), 1, 254)
    scaled = (w * np.exp2(127.0 - byte)[:, None, :]).reshape(k, n).astype(np.float32)
    words = np.ascontiguousarray(scaled.reshape(k // 512, 128, 4, n).transpose(0, 1, 3, 2)).astype(ml_dtypes.float8_e4m3fn).view(np.uint8)
    return words, np.ascontiguousarray(byte.astype(np.uint8).reshape(k // 512, 16, n))


def unpack_weight(words, scales):
    g, p, n, _ = words.shape
    vals = np.ascontiguousarray(words).view(ml_dtypes.float8_e4m3fn).astype(np.float64) * np.repeat(np.exp2(scales.astype(np.float64) - 127.0), 8, axis=1)[..., None]
    return vals.transpose(0, 1, 3, 2).reshape(g * 512, n)


def sigmoid(v):
    return 1.0 / (1.0 + np.exp(-np.maximum(v, -700.0)))


K, T, S, H, V, D, U = 512, 2048, 512, 512, 256, 2, 512


def setup_inputs():
    n = np.random.standard_normal
    s = mx_kscale(K)[:, None]
    u = mx_kscale(H)
    packed_xT = pack_weight(n((K, T)) * s)
    return {
        "x_words": packed_xT[0],
        "x_scales": packed_xT[1],
        "w1": (n((K, H)) / np.sqrt(K) / s).astype(np.float32),
        "paq": (np.random.uniform(0.0, 1.0, (H, V)) ** 2 / H * 4 / u[:, None]).astype(np.float32),
        "unit": (np.random.uniform(0.7, 1.3, (H, 1)) * u[:, None]).astype(np.float32),
        "offs": striped(np.random.permutation(T)[:S]),
        "shown": striped(np.random.permutation(T)[:U]),
    }


def reference(x_words, x_scales, w1, paq, unit, offs, shown):
    x_shown = unpack_weight(x_words, x_scales)[:, unstriped(shown)]
    w1q = mxq(f64(w1), 0, "e4m3")
    ps = sigmoid((w1q.T @ x_shown) - 1.0)
    lg = np.log(-1.0 * ps + 1.001)
    nov = np.exp(lg.reshape(len(lg), -1, D).sum(axis=2))
    z = nov * f64(paq)
    xq = unpack_weight(x_words, x_scales)[:, unstriped(offs)]
    pd = sigmoid(w1q.T @ xq)
    dd = f64(unit) * pd
    return np.log((mxq(z, 0, "e4m3").T @ mxq(dd, 0, "e4m3")) + 0.01)

@@ -1,0 +1,174 @@
+from contextlib import ExitStack
+
+import concourse.mybir as mybir
+
+K, T, S, H, V, D = 512, 2048, 512, 512, 256, 2
+FLOPS = 2 * K * H * S * 2 + 2 * H * V * S
+
+F32 = mybir.dt.float32
+BF16 = mybir.dt.bfloat16
+I32 = mybir.dt.int32
+U32 = mybir.dt.uint32
+U16 = mybir.dt.uint16
+U8 = mybir.dt.uint8
+FP8X4 = mybir.dt.float8_e4m3fn_x4
+ACT = mybir.ActivationFunctionType
+ALU = mybir.AluOpType
+
+P = 128
+PACK = 4
+COLS = 128
+HALF = 256
+
+
+def tile_picked_yxquad_log_p_kernel(tc, x_words, x_scales, w1, paq, unit, offs, shown, out):
+    nc = tc.nc
+    with ExitStack() as ctx:
+        keep = ctx.enter_context(tc.tile_pool(name="keep", bufs=1))
+        psum = ctx.enter_context(tc.psum_pool(name="psum", bufs=8))
+
+        def sb(name, shape, dtype):
+            return keep.tile(shape, dtype, name=name, align_bytes=64)
+
+        shown_list = sb("shown_list", [P, S // 16], U16)
+        cand_list = sb("cand_list", [P, S // 16], U16)
+        scale_table = sb("scale_table", [P, T], U8)
+        word_table = sb("word_table", [P, T], U32)
+        w_raw = [sb(f"w_raw{h}", [P, PACK, HALF], F32) for h in range(2)]
+        paq_sb = sb("paq_sb", [P, PACK, V], F32)
+        unit_sb = sb("unit_sb", [P, PACK], F32)
+
+        warm = sb("warm", [P, 2], F32)
+        nc.vector.memset(scale_table[:].bitcast(I32), 0)
+        nc.gpsimd.memset(warm[:, 0:1], 0.0)
+        nc.scalar.activation(warm[:, 1:2], warm[:, 0:1], ACT.Sigmoid)
+
+        w_rows = w1.rearrange("(p j) c -> p j c", j=PACK)
+        nc.sync.dma_start(shown_list[:], shown)
+        nc.sync.dma_start(cand_list[:], offs)
+        nc.sync.dma_start(w_raw[0][:], w_rows[:, :, 0:HALF])
+        for q in range(4):
+            nc.sync.dma_start(scale_table[32 * q : 32 * q + 4, :].bitcast(I32), x_scales[0, 4 * q : 4 * q + 4, :].bitcast(I32))
+        nc.sync.dma_start(w_raw[1][:], w_rows[:, :, HALF : 2 * HALF])
+        nc.sync.dma_start(word_table[:].bitcast(I32), x_words[0].rearrange("p c r -> p (c r)").bitcast(I32))
+        nc.sync.dma_start(paq_sb[:], paq.rearrange("(p t) v -> p t v", t=PACK))
+        nc.sync.dma_start(unit_sb[:], unit.rearrange("(p t) o -> p (t o)", t=PACK))
+
+        w_bf = sb("w_bf", [P, PACK, P, PACK], BF16)
+        for h in range(2):
+            nc.scalar.copy(
+                w_bf[:, :, 64 * h : 64 * h + 64, :].rearrange("p t m j -> p m j t"),
+                w_raw[h][:].rearrange("p j (m t) -> p m j t", t=PACK),
+            )
+
+        shown_scales = sb("shown_scales", [P, S], U8)
+        cand_scales = sb("cand_scales", [P, S], U8)
+        nc.vector.tensor_copy(shown_scales[:], scale_table[:].indirect(shown_list[:]))
+        nc.vector.tensor_copy(cand_scales[:], scale_table[:].indirect(cand_list[:]))
+
+        w_codes = sb("w_codes", [P, H], U32)
+        w_scales = sb("w_scales", [P, H], U8)
+        nc.vector.quantize_mx(out=w_codes[:].bitcast(FP8X4), scales=w_scales[:], in_=w_bf[:].rearrange("p t m j -> p (t m j)"))
+
+        shown_words = [sb(f"shown_words{h}", [P, HALF], U32) for h in range(2)]
+        cand_words = [sb(f"cand_words{h}", [P, HALF], U32) for h in range(2)]
+
+        def gather_words(dst, lst, h):
+            nc.vector.tensor_copy(dst[h][:], word_table[:].indirect(lst[:, 16 * h : 16 * h + 16]))
+
+        def first_product(words, scales, b):
+            bank = psum.tile([P, PACK, COLS], F32, name="bank")
+            lo = (b % 2) * COLS
+            for t in range(PACK):
+                nc.tensor.matmul_mx(
+                    out=bank[:, t, :],
+                    lhsT=w_codes[:, t * P : (t + 1) * P].bitcast(FP8X4),
+                    lhsT_scale=w_scales[:, t * P : (t + 1) * P],
+                    rhs=words[b // 2][:, lo : lo + COLS].bitcast(FP8X4),
+                    rhs_scale=scales[:, b * COLS : (b + 1) * COLS],
+                    start=True,
+                    stop=True,
+                )
+            return bank
+
+        nq = COLS // D
+        rest = [sb(f"rest{b}", [P, D, nq, PACK], F32) for b in range(4)]
+        part = [sb(f"part{b}", [P, nq, PACK], F32) for b in range(4)]
+        pd = [sb(f"pd{b}", [P, COLS, PACK], F32) for b in range(4)]
+        z_bf = sb("z_bf", [P, V * PACK], BF16)
+        dd_bf = [sb("dd_bf0", [P, 2 * COLS * PACK], BF16), sb("dd_bf1", [P, COLS * PACK], BF16), sb("dd_bf2", [P, COLS * PACK], BF16)]
+
+        def shown_sigmoid(b):
+            bank = first_product(shown_words, shown_scales, b)
+            nc.scalar.activation(rest[b][:], bank[:].rearrange("p t (v d) -> p d v t", d=D), ACT.Sigmoid, bias=1.0, scale=-1.0)
+
+        def cand_sigmoid(b):
+            bank = first_product(cand_words, cand_scales, b)
+            nc.scalar.activation(pd[b][:], bank[:].rearrange("p t j -> p j t"), ACT.Sigmoid)
+
+        def z_first(b):
+            nc.vector.scalar_tensor_tensor(
+                part[b][:], rest[b][:, 0], 0.001, paq_sb[:, :, b * nq : (b + 1) * nq].rearrange("p t v -> p v t"), ALU.add, ALU.mult
+            )
+
+        def z_second(b):
+            dst = z_bf[:, b * nq * PACK : (b + 1) * nq * PACK].rearrange("p (v t) -> p v t", t=PACK)
+            nc.vector.scalar_tensor_tensor(dst, rest[b][:, 1], 0.001, part[b][:], ALU.add, ALU.mult)
+
+        def dd_mul(b):
+            c, lo = (0, b * COLS * PACK) if b < 2 else (b - 1, 0)
+            dst = dd_bf[c][:, lo : lo + COLS * PACK].rearrange("p (j t) -> p j t", t=PACK)
+            nc.vector.tensor_tensor(dst, pd[b][:], unit_sb[:].unsqueeze(1).to_broadcast([P, COLS, PACK]), ALU.mult)
+
+        z_codes = sb("z_codes", [P, V], U32)
+        z_scales = sb("z_scales", [P, V], U8)
+        widths = [2 * COLS, COLS, COLS]
+        starts = [0, 2 * COLS, 3 * COLS]
+        dd_codes = [sb(f"dd_codes{c}", [P, widths[c]], U32) for c in range(3)]
+        dd_scales = [sb(f"dd_scales{c}", [P, widths[c]], U8) for c in range(3)]
+
+        def dd_quant(c):
+            nc.vector.quantize_mx(out=dd_codes[c][:].bitcast(FP8X4), scales=dd_scales[c][:], in_=dd_bf[c][:])
+
+        out_rows = out.rearrange("(h p) j -> p h j", p=P)
+
+        def finish(c):
+            n = widths[c]
+            bank = psum.tile([P, 2, n], F32, name="bank")
+            for h in range(2):
+                nc.tensor.matmul_mx(
+                    out=bank[:, h, :],
+                    lhsT=z_codes[:, h * P : (h + 1) * P].bitcast(FP8X4),
+                    lhsT_scale=z_scales[:, h * P : (h + 1) * P],
+                    rhs=dd_codes[c][:].bitcast(FP8X4),
+                    rhs_scale=dd_scales[c][:],
+                    start=True,
+                    stop=True,
+                )
+            res = sb(f"res{c}", [P, 2, n], F32)
+            nc.scalar.activation(res[:], bank[:], ACT.Ln, bias=0.01)
+            nc.sync.dma_start(out_rows[:, :, starts[c] : starts[c] + n], res[:])
+
+        gather_words(shown_words, shown_list, 0)
+        gather_words(shown_words, shown_list, 1)
+        gather_words(cand_words, cand_list, 0)
+        for b in range(4):
+            shown_sigmoid(b)
+        z_first(0)
+        gather_words(cand_words, cand_list, 1)
+        for b in range(4):
+            cand_sigmoid(b)
+        for b in range(1, 4):
+            z_first(b)
+            z_second(b - 1)
+        dd_mul(0)
+        z_second(3)
+        dd_mul(1)
+        nc.vector.quantize_mx(out=z_codes[:].bitcast(FP8X4), scales=z_scales[:], in_=z_bf[:])
+        dd_mul(2)
+        dd_quant(0)
+        dd_mul(3)
+        dd_quant(1)
+        dd_quant(2)
+        for c in range(3):
+            finish(c)

@@ -47,8 +47,8 @@ def tile_picked_yxquad_log_p_kernel(tc, x_words, x_scales, w1, paq, unit, offs, 
         nc.sync.dma_start(shown_list[:], shown)
         nc.sync.dma_start(cand_list[:], offs)
         nc.sync.dma_start(w_raw[0][:], w_rows[:, :, 0:HALF])
-        for q in range(4):
-            nc.sync.dma_start(scale_table[32 * q : 32 * q + 4, :].bitcast(I32), x_scales[0, 4 * q : 4 * q + 4, :].bitcast(I32))
+        for r in range(4):
+            nc.sync.dma_start(scale_table[r:P:32, :].bitcast(I32), x_scales[0, r:16:4, :].bitcast(I32))
         nc.sync.dma_start(w_raw[1][:], w_rows[:, :, HALF : 2 * HALF])
         nc.sync.dma_start(word_table[:].bitcast(I32), x_words[0].rearrange("p c r -> p (c r)").bitcast(I32))
         nc.sync.dma_start(paq_sb[:], paq.rearrange("(p t) v -> p t v", t=PACK))

@@ -3,7 +3,7 @@ from contextlib import ExitStack
 import concourse.mybir as mybir
 
 K, T, S, H, V, D = 512, 2048, 512, 512, 256, 2
-FLOPS = 2 * K * H * S * 2 + 2 * H * V * S
+FLOPS = 2 * (2 * K * H * S) + 2 * H * V * S
 
 F32 = mybir.dt.float32
 BF16 = mybir.dt.bfloat16
@@ -17,86 +17,110 @@ ALU = mybir.AluOpType
 
 P = 128
 PACK = 4
-COLS = 128
-HALF = 256
+QUADRANT = 32
+SCALE_ROWS = K // 32
+LIST_ROWS = 16
+PSUM_BANKS = 8
+DOCS = 128
+BANKS = S // DOCS
+QUERIES = DOCS // D
+GATHER = 2 * DOCS
+W_HALF = H // 2
+M_HALF = W_HALF // PACK
+NOVELTY_FLOOR = 0.001
+LOG_FLOOR = 0.01
+CHUNK_BANKS = [(0, 1), (2,), (3,)]
 
 
 def tile_picked_yxquad_log_p_kernel(tc, x_words, x_scales, w1, paq, unit, offs, shown, out):
     nc = tc.nc
     with ExitStack() as ctx:
         keep = ctx.enter_context(tc.tile_pool(name="keep", bufs=1))
-        psum = ctx.enter_context(tc.psum_pool(name="psum", bufs=8))
+        psum = ctx.enter_context(tc.psum_pool(name="psum", bufs=PSUM_BANKS))
 
         def sb(name, shape, dtype):
             return keep.tile(shape, dtype, name=name, align_bytes=64)
 
-        shown_list = sb("shown_list", [P, S // 16], U16)
-        cand_list = sb("cand_list", [P, S // 16], U16)
+        shown_list = sb("shown_list", [P, S // LIST_ROWS], U16)
+        cand_list = sb("cand_list", [P, S // LIST_ROWS], U16)
         scale_table = sb("scale_table", [P, T], U8)
         word_table = sb("word_table", [P, T], U32)
-        w_raw = [sb(f"w_raw{h}", [P, PACK, HALF], F32) for h in range(2)]
+        w_raw = [sb(f"w_raw{h}", [P, PACK, W_HALF], F32) for h in range(2)]
         paq_sb = sb("paq_sb", [P, PACK, V], F32)
         unit_sb = sb("unit_sb", [P, PACK], F32)
 
-        warm = sb("warm", [P, 2], F32)
         nc.vector.memset(scale_table[:].bitcast(I32), 0)
+
+        warm = sb("warm", [P, 2], F32)
         nc.gpsimd.memset(warm[:, 0:1], 0.0)
         nc.scalar.activation(warm[:, 1:2], warm[:, 0:1], ACT.Sigmoid)
 
         w_rows = w1.rearrange("(p j) c -> p j c", j=PACK)
-        nc.sync.dma_start(shown_list[:], shown)
         nc.sync.dma_start(cand_list[:], offs)
-        nc.sync.dma_start(w_raw[0][:], w_rows[:, :, 0:HALF])
+        nc.sync.dma_start(w_raw[0][:], w_rows[:, :, 0:W_HALF])
+        nc.sync.dma_start(shown_list[:], shown)
         for r in range(4):
-            nc.sync.dma_start(scale_table[r:P:32, :].bitcast(I32), x_scales[0, r:16:4, :].bitcast(I32))
-        nc.sync.dma_start(w_raw[1][:], w_rows[:, :, HALF : 2 * HALF])
+            nc.sync.dma_start(scale_table[r:P:QUADRANT, :].bitcast(I32), x_scales[0, r:SCALE_ROWS:4, :].bitcast(I32))
+        nc.sync.dma_start(w_raw[1][:], w_rows[:, :, W_HALF:H])
         nc.sync.dma_start(word_table[:].bitcast(I32), x_words[0].rearrange("p c r -> p (c r)").bitcast(I32))
-        nc.sync.dma_start(paq_sb[:], paq.rearrange("(p t) v -> p t v", t=PACK))
         nc.sync.dma_start(unit_sb[:], unit.rearrange("(p t) o -> p (t o)", t=PACK))
+        nc.sync.dma_start(paq_sb[:], paq.rearrange("(p t) v -> p t v", t=PACK))
 
         w_bf = sb("w_bf", [P, PACK, P, PACK], BF16)
-        for h in range(2):
-            nc.scalar.copy(
-                w_bf[:, :, 64 * h : 64 * h + 64, :].rearrange("p t m j -> p m j t"),
-                w_raw[h][:].rearrange("p j (m t) -> p m j t", t=PACK),
-            )
+        w_dst = w_bf[:].rearrange("p t m j -> p m j t")
+        w_src = [w_raw[h][:].rearrange("p j (m t) -> p m j t", t=PACK) for h in range(2)]
+        nc.scalar.copy(w_dst[:, 0:M_HALF], w_src[0])
+        for u in range(2):
+            nc.scalar.copy(w_dst[:, M_HALF:P, :, 2 * u : 2 * u + 2], w_src[1][:, :, :, 2 * u : 2 * u + 2])
 
         shown_scales = sb("shown_scales", [P, S], U8)
         cand_scales = sb("cand_scales", [P, S], U8)
-        nc.vector.tensor_copy(shown_scales[:], scale_table[:].indirect(shown_list[:]))
         nc.vector.tensor_copy(cand_scales[:], scale_table[:].indirect(cand_list[:]))
+        nc.vector.tensor_copy(shown_scales[:], scale_table[:].indirect(shown_list[:]))
 
         w_codes = sb("w_codes", [P, H], U32)
         w_scales = sb("w_scales", [P, H], U8)
-        nc.vector.quantize_mx(out=w_codes[:].bitcast(FP8X4), scales=w_scales[:], in_=w_bf[:].rearrange("p t m j -> p (t m j)"))
+        for u in range(2):
+            cols = slice(2 * u * P, (2 * u + 2) * P)
+            nc.vector.quantize_mx(
+                out=w_codes[:, cols].bitcast(FP8X4),
+                scales=w_scales[:, cols],
+                in_=w_bf[:, 2 * u : 2 * u + 2].rearrange("p t m j -> p (t m j)"),
+            )
 
-        shown_words = [sb(f"shown_words{h}", [P, HALF], U32) for h in range(2)]
-        cand_words = [sb(f"cand_words{h}", [P, HALF], U32) for h in range(2)]
+        shown_words = [sb(f"shown_words{g}", [P, GATHER], U32) for g in range(S // GATHER)]
+        cand_words = [sb(f"cand_words{g}", [P, GATHER], U32) for g in range(S // GATHER)]
 
-        def gather_words(dst, lst, h):
-            nc.vector.tensor_copy(dst[h][:], word_table[:].indirect(lst[:, 16 * h : 16 * h + 16]))
+        def gather_words(words, entries, g):
+            width = GATHER // LIST_ROWS
+            nc.vector.tensor_copy(words[g][:], word_table[:].indirect(entries[:, g * width : (g + 1) * width]))
 
         def first_product(words, scales, b):
-            bank = psum.tile([P, PACK, COLS], F32, name="bank")
-            lo = (b % 2) * COLS
+            bank = psum.tile([P, PACK, DOCS], F32, name="bank")
+            g, lo = divmod(b * DOCS, GATHER)
             for t in range(PACK):
                 nc.tensor.matmul_mx(
                     out=bank[:, t, :],
                     lhsT=w_codes[:, t * P : (t + 1) * P].bitcast(FP8X4),
                     lhsT_scale=w_scales[:, t * P : (t + 1) * P],
-                    rhs=words[b // 2][:, lo : lo + COLS].bitcast(FP8X4),
-                    rhs_scale=scales[:, b * COLS : (b + 1) * COLS],
+                    rhs=words[g][:, lo : lo + DOCS].bitcast(FP8X4),
+                    rhs_scale=scales[:, b * DOCS : (b + 1) * DOCS],
                     start=True,
                     stop=True,
                 )
             return bank
 
-        nq = COLS // D
-        rest = [sb(f"rest{b}", [P, D, nq, PACK], F32) for b in range(4)]
-        part = [sb(f"part{b}", [P, nq, PACK], F32) for b in range(4)]
-        pd = [sb(f"pd{b}", [P, COLS, PACK], F32) for b in range(4)]
+        rest = [sb(f"rest{b}", [P, D, QUERIES, PACK], F32) for b in range(BANKS)]
+        part = [sb(f"part{b}", [P, QUERIES, PACK], F32) for b in range(BANKS)]
+        pd = [sb(f"pd{b}", [P, DOCS, PACK], F32) for b in range(BANKS)]
         z_bf = sb("z_bf", [P, V * PACK], BF16)
-        dd_bf = [sb("dd_bf0", [P, 2 * COLS * PACK], BF16), sb("dd_bf1", [P, COLS * PACK], BF16), sb("dd_bf2", [P, COLS * PACK], BF16)]
+        z_codes = sb("z_codes", [P, V], U32)
+        z_scales = sb("z_scales", [P, V], U8)
+        chunks = range(len(CHUNK_BANKS))
+        widths = [len(banks) * DOCS for banks in CHUNK_BANKS]
+        dd_bf = [sb(f"dd_bf{c}", [P, widths[c] * PACK], BF16) for c in chunks]
+        dd_codes = [sb(f"dd_codes{c}", [P, widths[c]], U32) for c in chunks]
+        dd_scales = [sb(f"dd_scales{c}", [P, widths[c]], U8) for c in chunks]
 
         def shown_sigmoid(b):
             bank = first_product(shown_words, shown_scales, b)
@@ -107,35 +131,30 @@ def tile_picked_yxquad_log_p_kernel(tc, x_words, x_scales, w1, paq, unit, offs, 
             nc.scalar.activation(pd[b][:], bank[:].rearrange("p t j -> p j t"), ACT.Sigmoid)
 
         def z_first(b):
-            nc.vector.scalar_tensor_tensor(
-                part[b][:], rest[b][:, 0], 0.001, paq_sb[:, :, b * nq : (b + 1) * nq].rearrange("p t v -> p v t"), ALU.add, ALU.mult
-            )
+            weights = paq_sb[:, :, b * QUERIES : (b + 1) * QUERIES].rearrange("p t v -> p v t")
+            nc.vector.scalar_tensor_tensor(part[b][:], rest[b][:, 0], NOVELTY_FLOOR, weights, ALU.add, ALU.mult)
 
         def z_second(b):
-            dst = z_bf[:, b * nq * PACK : (b + 1) * nq * PACK].rearrange("p (v t) -> p v t", t=PACK)
-            nc.vector.scalar_tensor_tensor(dst, rest[b][:, 1], 0.001, part[b][:], ALU.add, ALU.mult)
+            dst = z_bf[:, b * QUERIES * PACK : (b + 1) * QUERIES * PACK].rearrange("p (v t) -> p v t", t=PACK)
+            nc.vector.scalar_tensor_tensor(dst, rest[b][:, 1], NOVELTY_FLOOR, part[b][:], ALU.add, ALU.mult)
 
-        def dd_mul(b):
-            c, lo = (0, b * COLS * PACK) if b < 2 else (b - 1, 0)
-            dst = dd_bf[c][:, lo : lo + COLS * PACK].rearrange("p (j t) -> p j t", t=PACK)
-            nc.vector.tensor_tensor(dst, pd[b][:], unit_sb[:].unsqueeze(1).to_broadcast([P, COLS, PACK]), ALU.mult)
+        def z_quant():
+            nc.vector.quantize_mx(out=z_codes[:].bitcast(FP8X4), scales=z_scales[:], in_=z_bf[:])
 
-        z_codes = sb("z_codes", [P, V], U32)
-        z_scales = sb("z_scales", [P, V], U8)
-        widths = [2 * COLS, COLS, COLS]
-        starts = [0, 2 * COLS, 3 * COLS]
-        dd_codes = [sb(f"dd_codes{c}", [P, widths[c]], U32) for c in range(3)]
-        dd_scales = [sb(f"dd_scales{c}", [P, widths[c]], U8) for c in range(3)]
+        def dd_mul(c, place):
+            b = CHUNK_BANKS[c][place]
+            dst = dd_bf[c][:, place * DOCS * PACK : (place + 1) * DOCS * PACK].rearrange("p (j t) -> p j t", t=PACK)
+            nc.vector.tensor_tensor(dst, pd[b][:], unit_sb[:].unsqueeze(1).to_broadcast([P, DOCS, PACK]), ALU.mult)
 
         def dd_quant(c):
             nc.vector.quantize_mx(out=dd_codes[c][:].bitcast(FP8X4), scales=dd_scales[c][:], in_=dd_bf[c][:])
 
         out_rows = out.rearrange("(h p) j -> p h j", p=P)
 
-        def finish(c):
-            n = widths[c]
-            bank = psum.tile([P, 2, n], F32, name="bank")
-            for h in range(2):
+        def second_product(c):
+            first = CHUNK_BANKS[c][0] * DOCS
+            bank = psum.tile([P, V // P, widths[c]], F32, name="bank")
+            for h in range(V // P):
                 nc.tensor.matmul_mx(
                     out=bank[:, h, :],
                     lhsT=z_codes[:, h * P : (h + 1) * P].bitcast(FP8X4),
@@ -145,30 +164,34 @@ def tile_picked_yxquad_log_p_kernel(tc, x_words, x_scales, w1, paq, unit, offs, 
                     start=True,
                     stop=True,
                 )
-            res = sb(f"res{c}", [P, 2, n], F32)
-            nc.scalar.activation(res[:], bank[:], ACT.Ln, bias=0.01)
-            nc.sync.dma_start(out_rows[:, :, starts[c] : starts[c] + n], res[:])
+            res = sb(f"res{c}", [P, V // P, widths[c]], F32)
+            nc.scalar.activation(res[:], bank[:], ACT.Ln, bias=LOG_FLOOR)
+            nc.sync.dma_start(out_rows[:, :, first : first + widths[c]], res[:])
 
+        gather_words(cand_words, cand_list, 0)
         gather_words(shown_words, shown_list, 0)
         gather_words(shown_words, shown_list, 1)
-        gather_words(cand_words, cand_list, 0)
-        for b in range(4):
-            shown_sigmoid(b)
-        z_first(0)
         gather_words(cand_words, cand_list, 1)
-        for b in range(4):
+        for b in CHUNK_BANKS[0]:
             cand_sigmoid(b)
-        for b in range(1, 4):
+        for b in range(BANKS):
+            shown_sigmoid(b)
+        for banks in CHUNK_BANKS[1:]:
+            cand_sigmoid(banks[0])
+
+        dd_mul(0, 0)
+        dd_mul(0, 1)
+        z_first(0)
+        dd_quant(0)
+        for b in range(1, BANKS):
             z_first(b)
             z_second(b - 1)
-        dd_mul(0)
-        z_second(3)
-        dd_mul(1)
-        nc.vector.quantize_mx(out=z_codes[:].bitcast(FP8X4), scales=z_scales[:], in_=z_bf[:])
-        dd_mul(2)
-        dd_quant(0)
-        dd_mul(3)
+        z_second(BANKS - 1)
+        dd_mul(1, 0)
+        z_quant()
+        dd_mul(2, 0)
         dd_quant(1)
         dd_quant(2)
-        for c in range(3):
-            finish(c)
+
+        for c in chunks:
+            second_product(c)

@@ -113,9 +113,10 @@ def tile_picked_yxquad_log_p_kernel(tc, x_words, x_scales, w1, paq, unit, offs, 
         rest = [sb(f"rest{b}", [P, D, QUERIES, PACK], F32) for b in range(BANKS)]
         part = [sb(f"part{b}", [P, QUERIES, PACK], F32) for b in range(BANKS)]
         pd = [sb(f"pd{b}", [P, DOCS, PACK], F32) for b in range(BANKS)]
-        z_bf = sb("z_bf", [P, V * PACK], BF16)
-        z_codes = sb("z_codes", [P, V], U32)
-        z_scales = sb("z_scales", [P, V], U8)
+        halves = range(V // P)
+        z_bf = [sb(f"z_bf{h}", [P, P * PACK], BF16) for h in halves]
+        z_codes = [sb(f"z_codes{h}", [P, P], U32) for h in halves]
+        z_scales = [sb(f"z_scales{h}", [P, P], U8) for h in halves]
         chunks = range(len(CHUNK_BANKS))
         widths = [len(banks) * DOCS for banks in CHUNK_BANKS]
         dd_bf = [sb(f"dd_bf{c}", [P, widths[c] * PACK], BF16) for c in chunks]
@@ -124,7 +125,8 @@ def tile_picked_yxquad_log_p_kernel(tc, x_words, x_scales, w1, paq, unit, offs, 
 
         def shown_sigmoid(b):
             bank = first_product(shown_words, shown_scales, b)
-            nc.scalar.activation(rest[b][:], bank[:].rearrange("p t (v d) -> p d v t", d=D), ACT.Sigmoid, bias=1.0, scale=-1.0)
+            dst = rest[b][:].rearrange("p d v t -> p v d t")
+            nc.scalar.activation(dst, bank[:].rearrange("p t (v d) -> p v d t", d=D), ACT.Sigmoid, bias=1.0, scale=-1.0)
 
         def cand_sigmoid(b):
             bank = first_product(cand_words, cand_scales, b)
@@ -135,11 +137,12 @@ def tile_picked_yxquad_log_p_kernel(tc, x_words, x_scales, w1, paq, unit, offs, 
             nc.vector.scalar_tensor_tensor(part[b][:], rest[b][:, 0], NOVELTY_FLOOR, weights, ALU.add, ALU.mult)
 
         def z_second(b):
-            dst = z_bf[:, b * QUERIES * PACK : (b + 1) * QUERIES * PACK].rearrange("p (v t) -> p v t", t=PACK)
+            h, lo = divmod(b * QUERIES, P)
+            dst = z_bf[h][:, lo * PACK : (lo + QUERIES) * PACK].rearrange("p (v t) -> p v t", t=PACK)
             nc.vector.scalar_tensor_tensor(dst, rest[b][:, 1], NOVELTY_FLOOR, part[b][:], ALU.add, ALU.mult)
 
-        def z_quant():
-            nc.vector.quantize_mx(out=z_codes[:].bitcast(FP8X4), scales=z_scales[:], in_=z_bf[:])
+        def z_quant(h):
+            nc.vector.quantize_mx(out=z_codes[h][:].bitcast(FP8X4), scales=z_scales[h][:], in_=z_bf[h][:])
 
         def dd_mul(c, place):
             b = CHUNK_BANKS[c][place]
@@ -151,22 +154,22 @@ def tile_picked_yxquad_log_p_kernel(tc, x_words, x_scales, w1, paq, unit, offs, 
 
         out_rows = out.rearrange("(h p) j -> p h j", p=P)
 
-        def second_product(c):
+        def second_product(c, hs):
             first = CHUNK_BANKS[c][0] * DOCS
-            bank = psum.tile([P, V // P, widths[c]], F32, name="bank")
-            for h in range(V // P):
+            bank = psum.tile([P, len(hs), widths[c]], F32, name="bank")
+            for place, h in enumerate(hs):
                 nc.tensor.matmul_mx(
-                    out=bank[:, h, :],
-                    lhsT=z_codes[:, h * P : (h + 1) * P].bitcast(FP8X4),
-                    lhsT_scale=z_scales[:, h * P : (h + 1) * P],
+                    out=bank[:, place, :],
+                    lhsT=z_codes[h][:].bitcast(FP8X4),
+                    lhsT_scale=z_scales[h][:],
                     rhs=dd_codes[c][:].bitcast(FP8X4),
                     rhs_scale=dd_scales[c][:],
                     start=True,
                     stop=True,
                 )
-            res = sb(f"res{c}", [P, V // P, widths[c]], F32)
+            res = sb(f"res{c}_{hs[0]}", [P, len(hs), widths[c]], F32)
             nc.scalar.activation(res[:], bank[:], ACT.Ln, bias=LOG_FLOOR)
-            nc.sync.dma_start(out_rows[:, :, first : first + widths[c]], res[:])
+            nc.sync.dma_start(out_rows[:, hs[0] : hs[-1] + 1, first : first + widths[c]], res[:])
 
         gather_words(cand_words, cand_list, 0)
         gather_words(shown_words, shown_list, 0)
@@ -187,11 +190,14 @@ def tile_picked_yxquad_log_p_kernel(tc, x_words, x_scales, w1, paq, unit, offs, 
             z_first(b)
             z_second(b - 1)
         z_second(BANKS - 1)
+        z_quant(0)
         dd_mul(1, 0)
-        z_quant()
+        z_quant(1)
         dd_mul(2, 0)
         dd_quant(1)
         dd_quant(2)
 
-        for c in chunks:
-            second_product(c)
+        for h in halves:
+            second_product(0, [h])
+        for c in chunks[1:]:
+            second_product(c, list(halves))

@@ -19,6 +19,7 @@ P = 128
 PACK = 4
 QUADRANT = 32
 SCALE_ROWS = K // 32
+ROW_STEP = P // SCALE_ROWS
 LIST_ROWS = 16
 PSUM_BANKS = 8
 DOCS = 128
@@ -38,45 +39,55 @@ def tile_picked_yxquad_log_p_kernel(tc, x_words, x_scales, w1, paq, unit, offs, 
         keep = ctx.enter_context(tc.tile_pool(name="keep", bufs=1))
         psum = ctx.enter_context(tc.psum_pool(name="psum", bufs=PSUM_BANKS))
 
-        def sb(name, shape, dtype):
-            return keep.tile(shape, dtype, name=name, align_bytes=64)
+        def sb(name, shape, dtype, after=None):
+            return keep.tile(shape, dtype, name=name, tag=after or name, align_bytes=64)
 
         shown_list = sb("shown_list", [P, S // LIST_ROWS], U16)
         cand_list = sb("cand_list", [P, S // LIST_ROWS], U16)
         scale_table = sb("scale_table", [P, T], U8)
         word_table = sb("word_table", [P, T], U32)
         w_raw = [sb(f"w_raw{h}", [P, PACK, W_HALF], F32) for h in range(2)]
-        paq_sb = sb("paq_sb", [P, PACK, V], F32)
-        unit_sb = sb("unit_sb", [P, PACK], F32)
 
         nc.vector.memset(scale_table[:].bitcast(I32), 0)
+        first_scales = sb("first_scales", [P, GATHER], U8)
+        nc.vector.memset(first_scales[:].bitcast(I32), 0)
 
         warm = sb("warm", [P, 2], F32)
         nc.gpsimd.memset(warm[:, 0:1], 0.0)
         nc.scalar.activation(warm[:, 1:2], warm[:, 0:1], ACT.Sigmoid)
 
         w_rows = w1.rearrange("(p j) c -> p j c", j=PACK)
-        nc.sync.dma_start(cand_list[:], offs)
         nc.sync.dma_start(w_raw[0][:], w_rows[:, :, 0:W_HALF])
+        nc.sync.dma_start(cand_list[:], offs)
         nc.sync.dma_start(shown_list[:], shown)
-        for r in range(4):
-            nc.sync.dma_start(scale_table[r:P:QUADRANT, :].bitcast(I32), x_scales[0, r:SCALE_ROWS:4, :].bitcast(I32))
+        nc.sync.dma_start(scale_table[0:P:ROW_STEP, :].bitcast(I32), x_scales[0].bitcast(I32))
         nc.sync.dma_start(w_raw[1][:], w_rows[:, :, W_HALF:H])
         nc.sync.dma_start(word_table[:].bitcast(I32), x_words[0].rearrange("p c r -> p (c r)").bitcast(I32))
-        nc.sync.dma_start(unit_sb[:], unit.rearrange("(p t) o -> p (t o)", t=PACK))
-        nc.sync.dma_start(paq_sb[:], paq.rearrange("(p t) v -> p t v", t=PACK))
 
-        w_bf = sb("w_bf", [P, PACK, P, PACK], BF16)
-        w_dst = w_bf[:].rearrange("p t m j -> p m j t")
-        w_src = [w_raw[h][:].rearrange("p j (m t) -> p m j t", t=PACK) for h in range(2)]
-        nc.scalar.copy(w_dst[:, 0:M_HALF], w_src[0])
-        for u in range(2):
-            nc.scalar.copy(w_dst[:, M_HALF:P, :, 2 * u : 2 * u + 2], w_src[1][:, :, :, 2 * u : 2 * u + 2])
+        w_bf = [sb(f"w_bf{u}", [P, 2, P, PACK], BF16) for u in range(2)]
+        for h in range(2):
+            w_src = w_raw[h][:].rearrange("p j (m t) -> p m j t", t=PACK)
+            for u in range(2):
+                w_dst = w_bf[u][:].rearrange("p t m j -> p m j t")
+                nc.scalar.copy(w_dst[:, h * M_HALF : (h + 1) * M_HALF], w_src[:, :, :, 2 * u : 2 * u + 2])
 
-        shown_scales = sb("shown_scales", [P, S], U8)
-        cand_scales = sb("cand_scales", [P, S], U8)
-        nc.vector.tensor_copy(cand_scales[:], scale_table[:].indirect(cand_list[:]))
-        nc.vector.tensor_copy(shown_scales[:], scale_table[:].indirect(shown_list[:]))
+        def move_rows(plane, picked, rows):
+            for r in rows:
+                nc.sync.dma_start(plane[r:P:QUADRANT, :].bitcast(I32), picked[r * ROW_STEP : P : QUADRANT, :].bitcast(I32))
+
+        first_cols = GATHER // LIST_ROWS
+        first_picked = sb("first_picked", [P, GATHER], U8)
+        later_picked = sb("later_picked", [P, 2 * S - GATHER], U8)
+        later_scales = sb("later_scales", [P, 2 * S - GATHER], U8)
+        nc.vector.tensor_copy(first_picked[:], scale_table[:].indirect(cand_list[:, 0:first_cols]))
+        move_rows(first_scales, first_picked, range(4))
+        nc.vector.tensor_copy(later_picked[:, 0:S], scale_table[:].indirect(shown_list[:]))
+        nc.vector.tensor_copy(later_picked[:, S:], scale_table[:].indirect(cand_list[:, first_cols:]))
+        nc.vector.tensor_copy(later_scales[:].bitcast(I32), later_picked[:].bitcast(I32))
+        move_rows(later_scales, later_picked, range(1, 4))
+        shown_scales = [later_scales[:, b * DOCS : (b + 1) * DOCS] for b in range(BANKS)]
+        cand_scales = [first_scales[:, b * DOCS : (b + 1) * DOCS] for b in range(GATHER // DOCS)]
+        cand_scales.extend(later_scales[:, S + b * DOCS : S + (b + 1) * DOCS] for b in range(BANKS - GATHER // DOCS))
 
         w_codes = sb("w_codes", [P, H], U32)
         w_scales = sb("w_scales", [P, H], U8)
@@ -85,8 +96,13 @@ def tile_picked_yxquad_log_p_kernel(tc, x_words, x_scales, w1, paq, unit, offs, 
             nc.vector.quantize_mx(
                 out=w_codes[:, cols].bitcast(FP8X4),
                 scales=w_scales[:, cols],
-                in_=w_bf[:, 2 * u : 2 * u + 2].rearrange("p t m j -> p (t m j)"),
+                in_=w_bf[u][:].rearrange("p t m j -> p (t m j)"),
             )
+
+        unit_sb = sb("unit_sb", [P, PACK], F32, after="w_bf0")
+        nc.sync.dma_start(unit_sb[:], unit.rearrange("(p t) o -> p (t o)", t=PACK))
+        paq_sb = sb("paq_sb", [P, PACK, V], F32, after="w_bf1")
+        nc.sync.dma_start(paq_sb[:], paq.rearrange("(p t) v -> p t v", t=PACK))
 
         shown_words = [sb(f"shown_words{g}", [P, GATHER], U32) for g in range(S // GATHER)]
         cand_words = [sb(f"cand_words{g}", [P, GATHER], U32) for g in range(S // GATHER)]
@@ -104,7 +120,7 @@ def tile_picked_yxquad_log_p_kernel(tc, x_words, x_scales, w1, paq, unit, offs, 
                     lhsT=w_codes[:, t * P : (t + 1) * P].bitcast(FP8X4),
                     lhsT_scale=w_scales[:, t * P : (t + 1) * P],
                     rhs=words[g][:, lo : lo + DOCS].bitcast(FP8X4),
-                    rhs_scale=scales[:, b * DOCS : (b + 1) * DOCS],
+                    rhs_scale=scales[b],
                     start=True,
                     stop=True,
                 )

@@ -49,8 +49,6 @@ def tile_picked_yxquad_log_p_kernel(tc, x_words, x_scales, w1, paq, unit, offs, 
         w_raw = [sb(f"w_raw{h}", [P, PACK, W_HALF], F32) for h in range(2)]
 
         nc.vector.memset(scale_table[:].bitcast(I32), 0)
-        first_scales = sb("first_scales", [P, GATHER], U8)
-        nc.vector.memset(first_scales[:].bitcast(I32), 0)
 
         warm = sb("warm", [P, 2], F32)
         nc.gpsimd.memset(warm[:, 0:1], 0.0)
@@ -59,9 +57,9 @@ def tile_picked_yxquad_log_p_kernel(tc, x_words, x_scales, w1, paq, unit, offs, 
         w_rows = w1.rearrange("(p j) c -> p j c", j=PACK)
         nc.sync.dma_start(w_raw[0][:], w_rows[:, :, 0:W_HALF])
         nc.sync.dma_start(cand_list[:], offs)
-        nc.sync.dma_start(shown_list[:], shown)
         nc.sync.dma_start(scale_table[0:P:ROW_STEP, :].bitcast(I32), x_scales[0].bitcast(I32))
         nc.sync.dma_start(w_raw[1][:], w_rows[:, :, W_HALF:H])
+        nc.sync.dma_start(shown_list[:], shown)
         nc.sync.dma_start(word_table[:].bitcast(I32), x_words[0].rearrange("p c r -> p (c r)").bitcast(I32))
 
         w_bf = [sb(f"w_bf{u}", [P, 2, P, PACK], BF16) for u in range(2)]
@@ -80,9 +78,11 @@ def tile_picked_yxquad_log_p_kernel(tc, x_words, x_scales, w1, paq, unit, offs, 
         later_picked = sb("later_picked", [P, 2 * S - GATHER], U8)
         later_scales = sb("later_scales", [P, 2 * S - GATHER], U8)
         nc.vector.tensor_copy(first_picked[:], scale_table[:].indirect(cand_list[:, 0:first_cols]))
-        move_rows(first_scales, first_picked, range(4))
-        nc.vector.tensor_copy(later_picked[:, 0:S], scale_table[:].indirect(shown_list[:]))
+        first_scales = sb("first_scales", [P, GATHER], U8)
+        nc.vector.tensor_copy(first_scales[:].bitcast(I32), first_picked[:].bitcast(I32))
+        move_rows(first_scales, first_picked, range(1, 4))
         nc.vector.tensor_copy(later_picked[:, S:], scale_table[:].indirect(cand_list[:, first_cols:]))
+        nc.vector.tensor_copy(later_picked[:, 0:S], scale_table[:].indirect(shown_list[:]))
         nc.vector.tensor_copy(later_scales[:].bitcast(I32), later_picked[:].bitcast(I32))
         move_rows(later_scales, later_picked, range(1, 4))
         shown_scales = [later_scales[:, b * DOCS : (b + 1) * DOCS] for b in range(BANKS)]
@@ -101,8 +101,9 @@ def tile_picked_yxquad_log_p_kernel(tc, x_words, x_scales, w1, paq, unit, offs, 
 
         unit_sb = sb("unit_sb", [P, PACK], F32, after="w_bf0")
         nc.sync.dma_start(unit_sb[:], unit.rearrange("(p t) o -> p (t o)", t=PACK))
-        paq_sb = sb("paq_sb", [P, PACK, V], F32, after="w_bf1")
-        nc.sync.dma_start(paq_sb[:], paq.rearrange("(p t) v -> p t v", t=PACK))
+        paq_sb = sb("paq_sb", [P, V // P, PACK, P], F32, after="w_bf1")
+        for h in range(V // P):
+            nc.sync.dma_start(paq_sb[:, h], paq.rearrange("(p t) v -> p t v", t=PACK)[:, :, h * P : (h + 1) * P])
 
         shown_words = [sb(f"shown_words{g}", [P, GATHER], U32) for g in range(S // GATHER)]
         cand_words = [sb(f"cand_words{g}", [P, GATHER], U32) for g in range(S // GATHER)]
@@ -149,7 +150,8 @@ def tile_picked_yxquad_log_p_kernel(tc, x_words, x_scales, w1, paq, unit, offs, 
             nc.scalar.activation(pd[b][:], bank[:].rearrange("p t j -> p j t"), ACT.Sigmoid)
 
         def z_first(b):
-            weights = paq_sb[:, :, b * QUERIES : (b + 1) * QUERIES].rearrange("p t v -> p v t")
+            h, lo = divmod(b * QUERIES, P)
+            weights = paq_sb[:, h, :, lo : lo + QUERIES].rearrange("p t v -> p v t")
             nc.vector.scalar_tensor_tensor(part[b][:], rest[b][:, 0], NOVELTY_FLOOR, weights, ALU.add, ALU.mult)
 
         def z_second(b):

@@ -49,6 +49,10 @@ def tile_picked_yxquad_log_p_kernel(tc, x_words, x_scales, w1, paq, unit, offs, 
         w_raw = [sb(f"w_raw{h}", [P, PACK, W_HALF], F32) for h in range(2)]
 
         nc.vector.memset(scale_table[:].bitcast(I32), 0)
+        first_scales = sb("first_scales", [P, GATHER], U8)
+        nc.vector.memset(first_scales[:].bitcast(I32), 0)
+        later_scales = sb("later_scales", [P, 2 * S - GATHER], U8)
+        nc.vector.memset(later_scales[:].bitcast(I32), 0)
 
         warm = sb("warm", [P, 2], F32)
         nc.gpsimd.memset(warm[:, 0:1], 0.0)
@@ -57,9 +61,9 @@ def tile_picked_yxquad_log_p_kernel(tc, x_words, x_scales, w1, paq, unit, offs, 
         w_rows = w1.rearrange("(p j) c -> p j c", j=PACK)
         nc.sync.dma_start(w_raw[0][:], w_rows[:, :, 0:W_HALF])
         nc.sync.dma_start(cand_list[:], offs)
+        nc.sync.dma_start(shown_list[:], shown)
         nc.sync.dma_start(scale_table[0:P:ROW_STEP, :].bitcast(I32), x_scales[0].bitcast(I32))
         nc.sync.dma_start(w_raw[1][:], w_rows[:, :, W_HALF:H])
-        nc.sync.dma_start(shown_list[:], shown)
         nc.sync.dma_start(word_table[:].bitcast(I32), x_words[0].rearrange("p c r -> p (c r)").bitcast(I32))
 
         w_bf = [sb(f"w_bf{u}", [P, 2, P, PACK], BF16) for u in range(2)]
@@ -76,15 +80,11 @@ def tile_picked_yxquad_log_p_kernel(tc, x_words, x_scales, w1, paq, unit, offs, 
         first_cols = GATHER // LIST_ROWS
         first_picked = sb("first_picked", [P, GATHER], U8)
         later_picked = sb("later_picked", [P, 2 * S - GATHER], U8)
-        later_scales = sb("later_scales", [P, 2 * S - GATHER], U8)
         nc.vector.tensor_copy(first_picked[:], scale_table[:].indirect(cand_list[:, 0:first_cols]))
-        first_scales = sb("first_scales", [P, GATHER], U8)
-        nc.vector.tensor_copy(first_scales[:].bitcast(I32), first_picked[:].bitcast(I32))
-        move_rows(first_scales, first_picked, range(1, 4))
+        move_rows(first_scales, first_picked, range(4))
         nc.vector.tensor_copy(later_picked[:, S:], scale_table[:].indirect(cand_list[:, first_cols:]))
         nc.vector.tensor_copy(later_picked[:, 0:S], scale_table[:].indirect(shown_list[:]))
-        nc.vector.tensor_copy(later_scales[:].bitcast(I32), later_picked[:].bitcast(I32))
-        move_rows(later_scales, later_picked, range(1, 4))
+        move_rows(later_scales, later_picked, range(4))
         shown_scales = [later_scales[:, b * DOCS : (b + 1) * DOCS] for b in range(BANKS)]
         cand_scales = [first_scales[:, b * DOCS : (b + 1) * DOCS] for b in range(GATHER // DOCS)]
         cand_scales.extend(later_scales[:, S + b * DOCS : S + (b + 1) * DOCS] for b in range(BANKS - GATHER // DOCS))

@@ -18,6 +18,7 @@ ALU = mybir.AluOpType
 P = 128
 PACK = 4
 QUADRANT = 32
+QUADRANT_ROWS = 4
 SCALE_ROWS = K // 32
 ROW_STEP = P // SCALE_ROWS
 LIST_ROWS = 16
@@ -46,19 +47,15 @@ def tile_picked_yxquad_log_p_kernel(tc, x_words, x_scales, w1, paq, unit, offs, 
         cand_list = sb("cand_list", [P, S // LIST_ROWS], U16)
         scale_table = sb("scale_table", [P, T], U8)
         word_table = sb("word_table", [P, T], U32)
-        w_raw = [sb(f"w_raw{h}", [P, PACK, W_HALF], F32) for h in range(2)]
+        w_raw = [sb(f"w_raw{load}", [P, PACK, W_HALF], F32) for load in range(2)]
 
         nc.vector.memset(scale_table[:].bitcast(I32), 0)
-        first_scales = sb("first_scales", [P, GATHER], U8)
-        nc.vector.memset(first_scales[:].bitcast(I32), 0)
-        later_scales = sb("later_scales", [P, 2 * S - GATHER], U8)
-        nc.vector.memset(later_scales[:].bitcast(I32), 0)
+        first_plane = sb("first_plane", [P, GATHER], U8)
+        nc.vector.memset(first_plane[:].bitcast(I32), 0)
+        later_plane = sb("later_plane", [P, 2 * S - GATHER], U8)
+        nc.vector.memset(later_plane[:].bitcast(I32), 0)
 
-        warm = sb("warm", [P, 2], F32)
-        nc.gpsimd.memset(warm[:, 0:1], 0.0)
-        nc.scalar.activation(warm[:, 1:2], warm[:, 0:1], ACT.Sigmoid)
-
-        w_rows = w1.rearrange("(p j) c -> p j c", j=PACK)
+        w_rows = w1.rearrange("(p a) c -> p a c", a=PACK)
         nc.sync.dma_start(w_raw[0][:], w_rows[:, :, 0:W_HALF])
         nc.sync.dma_start(cand_list[:], offs)
         nc.sync.dma_start(shown_list[:], shown)
@@ -67,27 +64,27 @@ def tile_picked_yxquad_log_p_kernel(tc, x_words, x_scales, w1, paq, unit, offs, 
         nc.sync.dma_start(word_table[:].bitcast(I32), x_words[0].rearrange("p c r -> p (c r)").bitcast(I32))
 
         w_bf = [sb(f"w_bf{u}", [P, 2, P, PACK], BF16) for u in range(2)]
-        for h in range(2):
-            w_src = w_raw[h][:].rearrange("p j (m t) -> p m j t", t=PACK)
+        for load in range(2):
+            w_src = w_raw[load][:].rearrange("p a (m t) -> p m a t", t=PACK)
             for u in range(2):
-                w_dst = w_bf[u][:].rearrange("p t m j -> p m j t")
-                nc.scalar.copy(w_dst[:, h * M_HALF : (h + 1) * M_HALF], w_src[:, :, :, 2 * u : 2 * u + 2])
+                w_dst = w_bf[u][:].rearrange("p e m a -> p m a e")
+                nc.scalar.copy(w_dst[:, load * M_HALF : (load + 1) * M_HALF], w_src[:, :, :, 2 * u : 2 * u + 2])
 
-        def move_rows(plane, picked, rows):
-            for r in rows:
+        def move_rows(plane, picked):
+            for r in range(QUADRANT_ROWS):
                 nc.sync.dma_start(plane[r:P:QUADRANT, :].bitcast(I32), picked[r * ROW_STEP : P : QUADRANT, :].bitcast(I32))
 
         first_cols = GATHER // LIST_ROWS
         first_picked = sb("first_picked", [P, GATHER], U8)
         later_picked = sb("later_picked", [P, 2 * S - GATHER], U8)
         nc.vector.tensor_copy(first_picked[:], scale_table[:].indirect(cand_list[:, 0:first_cols]))
-        move_rows(first_scales, first_picked, range(4))
+        move_rows(first_plane, first_picked)
         nc.vector.tensor_copy(later_picked[:, S:], scale_table[:].indirect(cand_list[:, first_cols:]))
         nc.vector.tensor_copy(later_picked[:, 0:S], scale_table[:].indirect(shown_list[:]))
-        move_rows(later_scales, later_picked, range(4))
-        shown_scales = [later_scales[:, b * DOCS : (b + 1) * DOCS] for b in range(BANKS)]
-        cand_scales = [first_scales[:, b * DOCS : (b + 1) * DOCS] for b in range(GATHER // DOCS)]
-        cand_scales.extend(later_scales[:, S + b * DOCS : S + (b + 1) * DOCS] for b in range(BANKS - GATHER // DOCS))
+        move_rows(later_plane, later_picked)
+        shown_scales = [later_plane[:, lo : lo + DOCS] for lo in range(0, S, DOCS)]
+        cand_scales = [first_plane[:, lo : lo + DOCS] for lo in range(0, GATHER, DOCS)]
+        cand_scales.extend(later_plane[:, lo : lo + DOCS] for lo in range(S, 2 * S - GATHER, DOCS))
 
         w_codes = sb("w_codes", [P, H], U32)
         w_scales = sb("w_scales", [P, H], U8)
@@ -96,31 +93,32 @@ def tile_picked_yxquad_log_p_kernel(tc, x_words, x_scales, w1, paq, unit, offs, 
             nc.vector.quantize_mx(
                 out=w_codes[:, cols].bitcast(FP8X4),
                 scales=w_scales[:, cols],
-                in_=w_bf[u][:].rearrange("p t m j -> p (t m j)"),
+                in_=w_bf[u][:].rearrange("p e m a -> p (e m a)"),
             )
 
         unit_sb = sb("unit_sb", [P, PACK], F32, after="w_bf0")
         nc.sync.dma_start(unit_sb[:], unit.rearrange("(p t) o -> p (t o)", t=PACK))
+        halves = range(V // P)
         paq_sb = sb("paq_sb", [P, V // P, PACK, P], F32, after="w_bf1")
-        for h in range(V // P):
+        for h in halves:
             nc.sync.dma_start(paq_sb[:, h], paq.rearrange("(p t) v -> p t v", t=PACK)[:, :, h * P : (h + 1) * P])
 
-        shown_words = [sb(f"shown_words{g}", [P, GATHER], U32) for g in range(S // GATHER)]
-        cand_words = [sb(f"cand_words{g}", [P, GATHER], U32) for g in range(S // GATHER)]
+        shown_words = [sb(f"shown_words{piece}", [P, GATHER], U32) for piece in range(S // GATHER)]
+        cand_words = [sb(f"cand_words{piece}", [P, GATHER], U32) for piece in range(S // GATHER)]
 
-        def gather_words(words, entries, g):
-            width = GATHER // LIST_ROWS
-            nc.vector.tensor_copy(words[g][:], word_table[:].indirect(entries[:, g * width : (g + 1) * width]))
+        def gather_words(words, entries, piece):
+            offsets = entries[:, piece * GATHER // LIST_ROWS : (piece + 1) * GATHER // LIST_ROWS]
+            nc.vector.tensor_copy(words[piece][:], word_table[:].indirect(offsets))
 
         def first_product(words, scales, b):
             bank = psum.tile([P, PACK, DOCS], F32, name="bank")
-            g, lo = divmod(b * DOCS, GATHER)
+            piece, lo = divmod(b * DOCS, GATHER)
             for t in range(PACK):
                 nc.tensor.matmul_mx(
                     out=bank[:, t, :],
                     lhsT=w_codes[:, t * P : (t + 1) * P].bitcast(FP8X4),
                     lhsT_scale=w_scales[:, t * P : (t + 1) * P],
-                    rhs=words[g][:, lo : lo + DOCS].bitcast(FP8X4),
+                    rhs=words[piece][:, lo : lo + DOCS].bitcast(FP8X4),
                     rhs_scale=scales[b],
                     start=True,
                     stop=True,
@@ -130,7 +128,6 @@ def tile_picked_yxquad_log_p_kernel(tc, x_words, x_scales, w1, paq, unit, offs, 
         rest = [sb(f"rest{b}", [P, D, QUERIES, PACK], F32) for b in range(BANKS)]
         part = [sb(f"part{b}", [P, QUERIES, PACK], F32) for b in range(BANKS)]
         pd = [sb(f"pd{b}", [P, DOCS, PACK], F32) for b in range(BANKS)]
-        halves = range(V // P)
         z_bf = [sb(f"z_bf{h}", [P, P * PACK], BF16) for h in halves]
         z_codes = [sb(f"z_codes{h}", [P, P], U32) for h in halves]
         z_scales = [sb(f"z_scales{h}", [P, P], U8) for h in halves]

@@ -29,7 +29,7 @@ QUERIES = DOCS // D
 GATHER = 2 * DOCS
 W_HALF = H // 2
 M_HALF = W_HALF // PACK
-NOVELTY_FLOOR = 0.001
+NOVELTY_FLOOR = 1.002
 LOG_FLOOR = 0.01
 CHUNK_BANKS = [(0, 1), (2,), (3,)]
 
@@ -106,9 +106,10 @@ def tile_picked_yxquad_log_p_kernel(tc, x_words, x_scales, w1, paq, unit, offs, 
         shown_words = [sb(f"shown_words{piece}", [P, GATHER], U32) for piece in range(S // GATHER)]
         cand_words = [sb(f"cand_words{piece}", [P, GATHER], U32) for piece in range(S // GATHER)]
 
-        def gather_words(words, entries, piece):
-            offsets = entries[:, piece * GATHER // LIST_ROWS : (piece + 1) * GATHER // LIST_ROWS]
-            nc.vector.tensor_copy(words[piece][:], word_table[:].indirect(offsets))
+        def gather_words(words, entries, piece, lo=0, n=GATHER):
+            first = piece * GATHER + lo
+            offsets = entries[:, first // LIST_ROWS : (first + n) // LIST_ROWS]
+            nc.vector.tensor_copy(words[piece][:, lo : lo + n], word_table[:].indirect(offsets))
 
         def first_product(words, scales, b):
             bank = psum.tile([P, PACK, DOCS], F32, name="bank")
@@ -140,11 +141,11 @@ def tile_picked_yxquad_log_p_kernel(tc, x_words, x_scales, w1, paq, unit, offs, 
         def shown_sigmoid(b):
             bank = first_product(shown_words, shown_scales, b)
             dst = rest[b][:].rearrange("p d v t -> p v d t")
-            nc.scalar.activation(dst, bank[:].rearrange("p t (v d) -> p v d t", d=D), ACT.Sigmoid, bias=1.0, scale=-1.0)
+            nc.scalar.activation(dst, bank[:].rearrange("p t (v d) -> p v d t", d=D), ACT.Tanh, bias=0.5, scale=-0.5)
 
         def cand_sigmoid(b):
             bank = first_product(cand_words, cand_scales, b)
-            nc.scalar.activation(pd[b][:], bank[:].rearrange("p t j -> p j t"), ACT.Sigmoid)
+            nc.scalar.activation(pd[b][:], bank[:].rearrange("p t j -> p j t"), ACT.Tanh, scale=0.5)
 
         def z_first(b):
             h, lo = divmod(b * QUERIES, P)
@@ -162,7 +163,7 @@ def tile_picked_yxquad_log_p_kernel(tc, x_words, x_scales, w1, paq, unit, offs, 
         def dd_mul(c, place):
             b = CHUNK_BANKS[c][place]
             dst = dd_bf[c][:, place * DOCS * PACK : (place + 1) * DOCS * PACK].rearrange("p (j t) -> p j t", t=PACK)
-            nc.vector.tensor_tensor(dst, pd[b][:], unit_sb[:].unsqueeze(1).to_broadcast([P, DOCS, PACK]), ALU.mult)
+            nc.vector.scalar_tensor_tensor(dst, pd[b][:], 1.0, unit_sb[:].unsqueeze(1).to_broadcast([P, DOCS, PACK]), ALU.add, ALU.mult)
 
         def dd_quant(c):
             nc.vector.quantize_mx(out=dd_codes[c][:].bitcast(FP8X4), scales=dd_scales[c][:], in_=dd_bf[c][:])
@@ -183,10 +184,11 @@ def tile_picked_yxquad_log_p_kernel(tc, x_words, x_scales, w1, paq, unit, offs, 
                     stop=True,
                 )
             res = sb(f"res{c}_{hs[0]}", [P, len(hs), widths[c]], F32)
-            nc.scalar.activation(res[:], bank[:], ACT.Ln, bias=LOG_FLOOR)
+            nc.scalar.activation(res[:], bank[:], ACT.Ln, bias=LOG_FLOOR, scale=0.125)
             nc.sync.dma_start(out_rows[:, hs[0] : hs[-1] + 1, first : first + widths[c]], res[:])
 
-        gather_words(cand_words, cand_list, 0)
+        gather_words(cand_words, cand_list, 0, 0, DOCS)
+        gather_words(cand_words, cand_list, 0, DOCS, DOCS)
         gather_words(shown_words, shown_list, 0)
         gather_words(shown_words, shown_list, 1)
         gather_words(cand_words, cand_list, 1)

@@ -96,7 +96,7 @@ def tile_picked_yxquad_log_p_kernel(tc, x_words, x_scales, w1, paq, unit, offs, 
                 in_=w_bf[u][:].rearrange("p e m a -> p (e m a)"),
             )
 
-        unit_sb = sb("unit_sb", [P, PACK], F32, after="w_bf0")
+        unit_sb = sb("unit_sb", [P, PACK], F32, after="w_raw0")
         nc.sync.dma_start(unit_sb[:], unit.rearrange("(p t) o -> p (t o)", t=PACK))
         halves = range(V // P)
         paq_sb = sb("paq_sb", [P, V // P, PACK, P], F32, after="w_bf1")

from contextlib import ExitStack

import concourse.mybir as mybir

K, T, S, H, V, D = 512, 2048, 512, 512, 256, 2
FLOPS = 2 * (2 * K * H * S) + 2 * H * V * S

F32 = mybir.dt.float32
BF16 = mybir.dt.bfloat16
I32 = mybir.dt.int32
U32 = mybir.dt.uint32
U16 = mybir.dt.uint16
U8 = mybir.dt.uint8
FP8X4 = mybir.dt.float8_e4m3fn_x4
ACT = mybir.ActivationFunctionType
ALU = mybir.AluOpType

P = 128
PACK = 4
QUADRANT = 32
QUADRANT_ROWS = 4
SCALE_ROWS = K // 32
ROW_STEP = P // SCALE_ROWS
LIST_ROWS = 16
PSUM_BANKS = 8
DOCS = 128
BANKS = S // DOCS
QUERIES = DOCS // D
GATHER = 2 * DOCS
W_HALF = H // 2
M_HALF = W_HALF // PACK
NOVELTY_FLOOR = 1.002
LOG_FLOOR = 0.01
CHUNK_BANKS = [(0, 1), (2,), (3,)]


def tile_picked_yxquad_log_p_kernel(tc, x_words, x_scales, w1, paq, unit, offs, shown, out):
    nc = tc.nc
    with ExitStack() as ctx:
        keep = ctx.enter_context(tc.tile_pool(name="keep", bufs=1))
        psum = ctx.enter_context(tc.psum_pool(name="psum", bufs=PSUM_BANKS))

        def sb(name, shape, dtype, after=None):
            return keep.tile(shape, dtype, name=name, tag=after or name, align_bytes=64)

        shown_list = sb("shown_list", [P, S // LIST_ROWS], U16)
        cand_list = sb("cand_list", [P, S // LIST_ROWS], U16)
        scale_table = sb("scale_table", [P, T], U8)
        word_table = sb("word_table", [P, T], U32)
        w_raw = [sb(f"w_raw{load}", [P, PACK, W_HALF], F32) for load in range(2)]

        nc.vector.memset(scale_table[:].bitcast(I32), 0)
        first_plane = sb("first_plane", [P, GATHER], U8)
        nc.vector.memset(first_plane[:].bitcast(I32), 0)
        later_plane = sb("later_plane", [P, 2 * S - GATHER], U8)
        nc.vector.memset(later_plane[:].bitcast(I32), 0)

        w_rows = w1.rearrange("(p a) c -> p a c", a=PACK)
        nc.sync.dma_start(w_raw[0][:], w_rows[:, :, 0:W_HALF])
        nc.sync.dma_start(cand_list[:], offs)
        nc.sync.dma_start(shown_list[:], shown)
        nc.sync.dma_start(scale_table[0:P:ROW_STEP, :].bitcast(I32), x_scales[0].bitcast(I32))
        nc.sync.dma_start(w_raw[1][:], w_rows[:, :, W_HALF:H])
        nc.sync.dma_start(word_table[:].bitcast(I32), x_words[0].rearrange("p c r -> p (c r)").bitcast(I32))

        w_bf = [sb(f"w_bf{u}", [P, 2, P, PACK], BF16) for u in range(2)]
        for load in range(2):
            w_src = w_raw[load][:].rearrange("p a (m t) -> p m a t", t=PACK)
            for u in range(2):
                w_dst = w_bf[u][:].rearrange("p e m a -> p m a e")
                nc.scalar.copy(w_dst[:, load * M_HALF : (load + 1) * M_HALF], w_src[:, :, :, 2 * u : 2 * u + 2])

        def move_rows(plane, picked):
            for r in range(QUADRANT_ROWS):
                nc.sync.dma_start(plane[r:P:QUADRANT, :].bitcast(I32), picked[r * ROW_STEP : P : QUADRANT, :].bitcast(I32))

        first_cols = GATHER // LIST_ROWS
        first_picked = sb("first_picked", [P, GATHER], U8)
        later_picked = sb("later_picked", [P, 2 * S - GATHER], U8)
        nc.vector.tensor_copy(first_picked[:], scale_table[:].indirect(cand_list[:, 0:first_cols]))
        move_rows(first_plane, first_picked)
        nc.vector.tensor_copy(later_picked[:, S:], scale_table[:].indirect(cand_list[:, first_cols:]))
        nc.vector.tensor_copy(later_picked[:, 0:S], scale_table[:].indirect(shown_list[:]))
        move_rows(later_plane, later_picked)
        shown_scales = [later_plane[:, lo : lo + DOCS] for lo in range(0, S, DOCS)]
        cand_scales = [first_plane[:, lo : lo + DOCS] for lo in range(0, GATHER, DOCS)]
        cand_scales.extend(later_plane[:, lo : lo + DOCS] for lo in range(S, 2 * S - GATHER, DOCS))

        w_codes = sb("w_codes", [P, H], U32)
        w_scales = sb("w_scales", [P, H], U8)
        for u in range(2):
            cols = slice(2 * u * P, (2 * u + 2) * P)
            nc.vector.quantize_mx(
                out=w_codes[:, cols].bitcast(FP8X4),
                scales=w_scales[:, cols],
                in_=w_bf[u][:].rearrange("p e m a -> p (e m a)"),
            )

        unit_sb = sb("unit_sb", [P, PACK], F32, after="w_raw0")
        nc.sync.dma_start(unit_sb[:], unit.rearrange("(p t) o -> p (t o)", t=PACK))
        halves = range(V // P)
        paq_sb = sb("paq_sb", [P, V // P, PACK, P], F32, after="w_bf1")
        for h in halves:
            nc.sync.dma_start(paq_sb[:, h], paq.rearrange("(p t) v -> p t v", t=PACK)[:, :, h * P : (h + 1) * P])

        shown_words = [sb(f"shown_words{piece}", [P, GATHER], U32) for piece in range(S // GATHER)]
        cand_words = [sb(f"cand_words{piece}", [P, GATHER], U32) for piece in range(S // GATHER)]

        def gather_words(words, entries, piece, lo=0, n=GATHER):
            first = piece * GATHER + lo
            offsets = entries[:, first // LIST_ROWS : (first + n) // LIST_ROWS]
            nc.vector.tensor_copy(words[piece][:, lo : lo + n], word_table[:].indirect(offsets))

        def first_product(words, scales, b):
            bank = psum.tile([P, PACK, DOCS], F32, name="bank")
            piece, lo = divmod(b * DOCS, GATHER)
            for t in range(PACK):
                nc.tensor.matmul_mx(
                    out=bank[:, t, :],
                    lhsT=w_codes[:, t * P : (t + 1) * P].bitcast(FP8X4),
                    lhsT_scale=w_scales[:, t * P : (t + 1) * P],
                    rhs=words[piece][:, lo : lo + DOCS].bitcast(FP8X4),
                    rhs_scale=scales[b],
                    start=True,
                    stop=True,
                )
            return bank

        rest = [sb(f"rest{b}", [P, D, QUERIES, PACK], F32) for b in range(BANKS)]
        part = [sb(f"part{b}", [P, QUERIES, PACK], F32) for b in range(BANKS)]
        pd = [sb(f"pd{b}", [P, DOCS, PACK], F32) for b in range(BANKS)]
        z_bf = [sb(f"z_bf{h}", [P, P * PACK], BF16) for h in halves]
        z_codes = [sb(f"z_codes{h}", [P, P], U32) for h in halves]
        z_scales = [sb(f"z_scales{h}", [P, P], U8) for h in halves]
        chunks = range(len(CHUNK_BANKS))
        widths = [len(banks) * DOCS for banks in CHUNK_BANKS]
        dd_bf = [sb(f"dd_bf{c}", [P, widths[c] * PACK], BF16) for c in chunks]
        dd_codes = [sb(f"dd_codes{c}", [P, widths[c]], U32) for c in chunks]
        dd_scales = [sb(f"dd_scales{c}", [P, widths[c]], U8) for c in chunks]

        def shown_sigmoid(b):
            bank = first_product(shown_words, shown_scales, b)
            dst = rest[b][:].rearrange("p d v t -> p v d t")
            nc.scalar.activation(dst, bank[:].rearrange("p t (v d) -> p v d t", d=D), ACT.Tanh, bias=0.5, scale=-0.5)

        def cand_sigmoid(b):
            bank = first_product(cand_words, cand_scales, b)
            nc.scalar.activation(pd[b][:], bank[:].rearrange("p t j -> p j t"), ACT.Tanh, scale=0.5)

        def z_first(b):
            h, lo = divmod(b * QUERIES, P)
            weights = paq_sb[:, h, :, lo : lo + QUERIES].rearrange("p t v -> p v t")
            nc.vector.scalar_tensor_tensor(part[b][:], rest[b][:, 0], NOVELTY_FLOOR, weights, ALU.add, ALU.mult)

        def z_second(b):
            h, lo = divmod(b * QUERIES, P)
            dst = z_bf[h][:, lo * PACK : (lo + QUERIES) * PACK].rearrange("p (v t) -> p v t", t=PACK)
            nc.vector.scalar_tensor_tensor(dst, rest[b][:, 1], NOVELTY_FLOOR, part[b][:], ALU.add, ALU.mult)

        def z_quant(h):
            nc.vector.quantize_mx(out=z_codes[h][:].bitcast(FP8X4), scales=z_scales[h][:], in_=z_bf[h][:])

        def dd_mul(c, place):
            b = CHUNK_BANKS[c][place]
            dst = dd_bf[c][:, place * DOCS * PACK : (place + 1) * DOCS * PACK].rearrange("p (j t) -> p j t", t=PACK)
            nc.vector.scalar_tensor_tensor(dst, pd[b][:], 1.0, unit_sb[:].unsqueeze(1).to_broadcast([P, DOCS, PACK]), ALU.add, ALU.mult)

        def dd_quant(c):
            nc.vector.quantize_mx(out=dd_codes[c][:].bitcast(FP8X4), scales=dd_scales[c][:], in_=dd_bf[c][:])

        out_rows = out.rearrange("(h p) j -> p h j", p=P)

        def second_product(c, hs):
            first = CHUNK_BANKS[c][0] * DOCS
            bank = psum.tile([P, len(hs), widths[c]], F32, name="bank")
            for place, h in enumerate(hs):
                nc.tensor.matmul_mx(
                    out=bank[:, place, :],
                    lhsT=z_codes[h][:].bitcast(FP8X4),
                    lhsT_scale=z_scales[h][:],
                    rhs=dd_codes[c][:].bitcast(FP8X4),
                    rhs_scale=dd_scales[c][:],
                    start=True,
                    stop=True,
                )
            res = sb(f"res{c}_{hs[0]}", [P, len(hs), widths[c]], F32)
            nc.scalar.activation(res[:], bank[:], ACT.Ln, bias=LOG_FLOOR, scale=0.125)
            nc.sync.dma_start(out_rows[:, hs[0] : hs[-1] + 1, first : first + widths[c]], res[:])

        gather_words(cand_words, cand_list, 0, 0, DOCS)
        gather_words(cand_words, cand_list, 0, DOCS, DOCS)
        gather_words(shown_words, shown_list, 0)
        gather_words(shown_words, shown_list, 1)
        gather_words(cand_words, cand_list, 1)
        for b in CHUNK_BANKS[0]:
            cand_sigmoid(b)
        for b in range(BANKS):
            shown_sigmoid(b)
        for banks in CHUNK_BANKS[1:]:
            cand_sigmoid(banks[0])

        dd_mul(0, 0)
        dd_mul(0, 1)
        z_first(0)
        dd_quant(0)
        for b in range(1, BANKS):
            z_first(b)
            z_second(b - 1)
        z_second(BANKS - 1)
        z_quant(0)
        dd_mul(1, 0)
        z_quant(1)
        dd_mul(2, 0)
        dd_quant(1)
        dd_quant(2)

        for h in halves:
            second_product(0, [h])
        for c in chunks[1:]:
            second_product(c, list(halves))
